import numpy as np
import ml_dtypes


def mxq(x, axis, fmt="e4m3"):
    dtype, down = {"e4m3": (ml_dtypes.float8_e4m3fn, 7), "e5m2": (ml_dtypes.float8_e5m2, 14)}[fmt]
    v = np.moveaxis(np.asarray(x, np.float32).astype(ml_dtypes.bfloat16).astype(np.float64), axis, -1)
    blocks = v.reshape(v.shape[:-1] + (-1, 32))
    amax = np.abs(blocks).max(-1, keepdims=True)
    byte = np.maximum(np.where(amax > 0, np.frexp(amax)[1] - 1 + 127, 0) - down, 1)
    scale = np.exp2(byte - 127.0)
    codes = (blocks / scale).astype(np.float32).astype(dtype).astype(np.float64)
    return np.moveaxis((codes * scale).reshape(v.shape), -1, axis)


WIDE = False


def mx_kscale(k):
    if not WIDE:
        return np.ones(k)
    levels = np.array([10, -10, 5, -5, 0])
    if k % 512:
        return np.exp2(np.random.permutation(np.resize(levels, k // 32))).repeat(32)
    a = np.empty((k // 512, 16))
    for p in range(k // 512):
        a[p, :8] = np.random.permutation(np.resize(levels, 8))
        for g in range(8):
            far = levels[np.abs(levels - a[p, g]) >= 10]
            a[p, g + 8] = far[np.random.randint(len(far))]
    return np.exp2(a.ravel()).repeat(32)


def f64(x):
    return np.asarray(x).astype(np.float64)


def striped(idx):
    return np.tile(idx.reshape(-1, 16).T, (8, 1)).astype(np.uint16)


def unstriped(offs):
    return offs[:16].T.reshape(-1).astype(np.int64)


def striped8(idx):
    return np.concatenate([x.reshape(-1, 16).T for x in idx]).astype(np.uint16)


def runs(offs, k):
    lists = np.stack([offs[16 * r : 16 * r + 16].T.reshape(-1) for r in range(8)]).astype(np.int64)
    return lists[np.arange(k) % 512 // 64]


def pack_weight(w):
    k, n = w.shape
    w = f64(np.asarray(w, np.float32).astype(ml_dtypes.bfloat16)).reshape(k // 32, 32, n)
    amax = np.abs(w).max(1)
    byte = np.clip(np.where(amax > 0, np.frexp(amax)[1] - 1 + 127 - 7, 1), 1, 254)
    scaled = (w * np.exp2(127.0 - byte)[:, None, :]).reshape(k, n).astype(np.float32)
    words = np.ascontiguousarray(scaled.reshape(k // 512, 128, 4, n).transpose(0, 1, 3, 2)).astype(ml_dtypes.float8_e4m3fn).view(np.uint8)
    return words, np.ascontiguousarray(byte.astype(np.uint8).reshape(k // 512, 16, n))


def unpack_weight(words, scales):
    g, p, n, _ = words.shape
    vals = np.ascontiguousarray(words).view(ml_dtypes.float8_e4m3fn).astype(np.float64) * np.repeat(np.exp2(scales.astype(np.float64) - 127.0), 8, axis=1)[..., None]
    return vals.transpose(0, 1, 3, 2).reshape(g * 512, n)


def sigmoid(v):
    return 1.0 / (1.0 + np.exp(-np.maximum(v, -700.0)))


K, T, S, N, H = 512, 2048, 512, 512, 512


def setup_inputs():
    n = np.random.standard_normal
    s = mx_kscale(K)[:, None]
    u = mx_kscale(H)
    packed_xT = pack_weight(n((K, T)) * s)
    return {
        "x_words": packed_xT[0],
        "x_scales": packed_xT[1],
        "w1": (n((K, H)) / np.sqrt(K) / s).astype(np.float32),
        "gn": (np.random.uniform(0.5, 1.5, (H, 1)) * u[:, None]).astype(np.float32),
        "w2": (n((H, N)) / np.sqrt(H) / u[:, None]).astype(np.float32),
        "offs": striped(np.random.permutation(T)[:S]),
        "n1": striped8(np.stack([np.random.permutation(S) for _ in range(8)])),
        "n2": striped8(np.stack([np.random.permutation(S) for _ in range(8)])),
        "n3": striped8(np.stack([np.random.permutation(S) for _ in range(8)])),
        "n4": striped8(np.stack([np.random.permutation(S) for _ in range(8)])),
        "n5": striped8(np.stack([np.random.permutation(S) for _ in range(8)])),
        "n6": striped8(np.stack([np.random.permutation(S) for _ in range(8)])),
    }


def reference(x_words, x_scales, w1, gn, w2, offs, n1, n2, n3, n4, n5, n6):
    xq = unpack_weight(x_words, x_scales)[:, unstriped(offs)]
    y = mxq(f64(w1), 0, "e4m3").T @ xq
    pa = y[np.arange(H)[:, None], runs(n1, H)]
    z = f64(gn) * (pa + (sigmoid(y[np.arange(H)[:, None], runs(n2, H)])) * (y[np.arange(H)[:, None], runs(n3, H)] - pa))
    h = mxq(f64(w2), 0, "e4m3").T @ mxq(z, 0, "e4m3")
    return y * (h[np.arange(N)[:, None], runs(n4, N)] - h) + 0.5 * ((y[np.arange(H)[:, None], runs(n6, H)]) * (h[np.arange(N)[:, None], runs(n5, N)] - h))

@@ -1,0 +1,198 @@
+from contextlib import ExitStack
+
+import concourse.mybir as mybir
+
+K, T, S, N, H = 512, 2048, 512, 512, 512
+FLOPS = 2 * K * H * S + 2 * H * N * S
+
+F32 = mybir.dt.float32
+BF16 = mybir.dt.bfloat16
+I32 = mybir.dt.int32
+U32 = mybir.dt.uint32
+U16 = mybir.dt.uint16
+U8 = mybir.dt.uint8
+FP8X4 = mybir.dt.float8_e4m3fn_x4
+ACT = mybir.ActivationFunctionType
+ALU = mybir.AluOpType
+
+P = 128
+PACK = 4
+HALF = S // 2
+WIN = 2 * S
+
+
+def tile_picked_skipflowblerp_none_p_kernel(
+    tc, x_words, x_scales, w1, gn, w2, offs, n1, n2, n3, n4, n5, n6, out
+):
+    nc = tc.nc
+    with ExitStack() as ctx:
+        keep = ctx.enter_context(tc.tile_pool(name="keep", bufs=1))
+        work = ctx.enter_context(tc.tile_pool(name="work", bufs=4))
+        psum = ctx.enter_context(tc.psum_pool(name="psum", bufs=8))
+
+        def load_list(name, src):
+            lst = keep.tile([P, S // 16], U16, name=name)
+            nc.sync.dma_start(lst[:], src)
+            return lst
+
+        x_all = keep.tile([P, T], U32, name="x_all")
+        nc.sync.dma_start(x_all[:].bitcast(I32), x_words[0].rearrange("p n t -> p (n t)").bitcast(I32))
+        offs_l = load_list("offs_l", offs)
+        xs_all = keep.tile([P, T], U8, name="xs_all")
+        nc.vector.memset(xs_all[:].bitcast(I32), 0)
+        for q in range(4):
+            nc.scalar.dma_start(
+                xs_all[32 * q : 32 * q + 4, :].bitcast(I32), x_scales[0, 4 * q : 4 * q + 4, :].bitcast(I32)
+            )
+        w1_raw = [keep.tile([P, PACK, H // 2], F32, name="w1_raw%d" % c) for c in range(2)]
+        for c in range(2):
+            nc.sync.dma_start(w1_raw[c][:], w1.rearrange("(p j) c -> p j c", j=PACK)[:, :, c * (H // 2) : (c + 1) * (H // 2)])
+        n2_l = load_list("n2_l", n2)
+        n3_l = load_list("n3_l", n3)
+        n1_l = load_list("n1_l", n1)
+        gain = keep.tile([P, PACK], F32, name="gain")
+        nc.sync.dma_start(gain[:], gn.rearrange("(p t) o -> p (t o)", t=PACK))
+        w2_raw = keep.tile([P, PACK, N], F32, name="w2_raw")
+        nc.sync.dma_start(w2_raw[:], w2.rearrange("(p j) c -> p j c", j=PACK))
+        n4_l = load_list("n4_l", n4)
+        n5_l = load_list("n5_l", n5)
+        n6_l = load_list("n6_l", n6)
+
+        warm = keep.tile([P, 2], F32, name="warm")
+        nc.vector.memset(warm[:, 0:1], 0.0)
+        nc.scalar.activation(warm[:, 1:2], warm[:, 0:1], ACT.Sigmoid)
+
+        y_win = [keep.tile([P, WIN], F32, name="y_win%d" % t) for t in range(PACK)]
+        h_win = [keep.tile([P, WIN], F32, name="h_win%d" % t) for t in range(PACK)]
+        h_last = keep.tile([P, S], F32, name="h_last")
+        h_flat = [h_win[t + 1][:, S:] for t in range(PACK - 1)] + [h_last[:]]
+        for win in y_win + h_win[:1]:
+            nc.vector.memset(win[:, S:], 0.0)
+
+        xs_pick = keep.tile([P, S], U8, name="xs_pick", align_bytes=64)
+        nc.vector.tensor_copy(xs_pick[:], xs_all[:].indirect(offs_l[:]))
+        x_pick = keep.tile([P, S], U32, name="x_pick", align_bytes=64)
+        nc.vector.tensor_copy(x_pick[:], x_all[:].indirect(offs_l[:]))
+
+        neg_gain = keep.tile([P, PACK], F32, name="neg_gain")
+        nc.vector.tensor_scalar(neg_gain[:], gain[:], -1.0, None, ALU.mult)
+
+        def round_pair(name, raw, u, copy):
+            dealt = keep.tile([P, 2, P, PACK], BF16, name="%s_bf%d" % (name, u), align_bytes=64)
+            src = raw[:].rearrange("p j (m t) -> p m j t", t=PACK)[:, :, :, 2 * u : 2 * u + 2]
+            copy(dealt[:].rearrange("p t m j -> p m j t"), src)
+            return dealt
+
+        def quantise(name, grouped, width):
+            codes = keep.tile([P, width], U32, name=name + "_codes", align_bytes=64)
+            scales = keep.tile([P, width], U8, name=name + "_scales", align_bytes=64)
+            nc.vector.quantize_mx(out=codes[:].bitcast(FP8X4), scales=scales[:], in_=grouped)
+            return codes, scales
+
+        def product(acc, weights, t, codes, scales):
+            w_codes, w_scales = weights[t // 2]
+            cols = slice((t % 2) * P, (t % 2 + 1) * P)
+            nc.tensor.matmul_mx(
+                out=acc, lhsT=w_codes[:, cols].bitcast(FP8X4), lhsT_scale=w_scales[:, cols],
+                rhs=codes[:].bitcast(FP8X4), rhs_scale=scales[:], start=True, stop=True,
+            )
+
+        flat = "p t m j -> p (t m j)"
+        w1_bf = [keep.tile([P, 2, P, PACK], BF16, name="w1_bf%d" % u, align_bytes=64) for u in range(2)]
+
+        def round_w1(c, u):
+            src = w1_raw[c][:].rearrange("p j (m t) -> p m j t", t=PACK)[:, :, :, 2 * u : 2 * u + 2]
+            dst = w1_bf[u][:, :, c * (P // 2) : (c + 1) * (P // 2), :]
+            nc.vector.tensor_copy(dst.rearrange("p t m j -> p m j t"), src)
+
+        round_w1(0, 0)
+        round_w1(0, 1)
+        round_w1(1, 0)
+        w1_q = []
+        for t in range(PACK):
+            if t == 1:
+                round_w1(1, 1)
+            w1_q.append(quantise("w1_%d" % t, w1_bf[t // 2][:, t % 2].rearrange("p m j -> p (m j)"), P))
+            y_acc = psum.tile([P, S], F32, name="acc")
+            w_codes, w_scales = w1_q[t]
+            nc.tensor.matmul_mx(
+                out=y_acc[:], lhsT=w_codes[:].bitcast(FP8X4), lhsT_scale=w_scales[:],
+                rhs=x_pick[:].bitcast(FP8X4), rhs_scale=xs_pick[:], start=True, stop=True,
+            )
+            nc.scalar.copy(y_win[t][:, :S], y_acc[:])
+
+        w2_q = []
+
+        z_planes = keep.tile([P, PACK, S], BF16, name="z_planes")
+        pend = []
+
+        def blend(t, halves):
+            width = HALF * len(halves)
+            cols = slice(halves[0] * HALF // 16, (halves[-1] + 1) * HALF // 16)
+            gate = work.tile([P, width], F32, name="gate")
+            nc.scalar.activation(gate[:], y_win[t][:].indirect(n2_l[:, cols]), ACT.Sigmoid)
+            rest = work.tile([P, width], F32, name="rest")
+            nc.scalar.activation(rest[:], gate[:], ACT.Identity, bias=gain[:, t : t + 1], scale=neg_gain[:, t : t + 1])
+            far = work.tile([P, width], F32, name="far")
+            nc.vector.tensor_tensor(far[:], y_win[t][:].indirect(n3_l[:, cols]), gate[:], ALU.mult)
+            flush()
+            near = work.tile([P, width], F32, name="near")
+            nc.vector.tensor_tensor(near[:], y_win[t][:].indirect(n1_l[:, cols]), rest[:], ALU.mult)
+            pend.append((t, halves, far, near))
+
+        def flush():
+            for t, halves, far, near in pend:
+                part = slice(halves[0] * HALF, (halves[-1] + 1) * HALF)
+                nc.vector.scalar_tensor_tensor(
+                    z_planes[:, t, part], far[:], gain[:, t : t + 1], near[:], ALU.mult, ALU.add
+                )
+            pend.clear()
+
+        def second(half, planes, copy):
+            z_bf = keep.tile([P, HALF, PACK], BF16, name="z_bf%d" % half, align_bytes=64)
+            copy(
+                z_bf[:].rearrange("p (c i) t -> p c t i", i=4),
+                planes.rearrange("p t (c i) -> p c t i", i=4),
+            )
+            z_codes, z_scales = quantise("z%d" % half, z_bf[:].rearrange("p c t -> p (c t)"), HALF)
+            cols = slice(half * HALF, (half + 1) * HALF)
+            for t in range(PACK):
+                h_acc = psum.tile([P, HALF], F32, name="acc")
+                product(h_acc[:], w2_q, t, z_codes, z_scales)
+                nc.scalar.copy(h_win[t][:, cols], h_acc[:])
+                nc.scalar.copy(h_flat[t][:, cols], h_acc[:])
+
+        blend(0, [0])
+        blend(0, [1])
+        blend(1, [0, 1])
+        w2_bf = [round_pair("w2", w2_raw, 0, nc.vector.tensor_copy), round_pair("w2", w2_raw, 1, nc.scalar.copy)]
+        w2_q.extend([quantise("w2_%d" % u, w2_bf[u][:].rearrange(flat), 2 * P) for u in range(2)])
+        blend(2, [0, 1])
+        blend(3, [0])
+        blend(3, [1])
+        flush()
+        second(0, z_planes[:, :, :HALF], nc.scalar.copy)
+        second(1, z_planes[:, :, HALF:], nc.vector.tensor_copy)
+
+        out_rows = out.rearrange("(p t) j -> t p j", t=PACK)
+        pend = []
+        for t in range(PACK):
+            d5 = work.tile([P, S], F32, name="d5")
+            nc.vector.tensor_tensor(d5[:], h_win[t][:].indirect(n5_l[:]), h_flat[t], ALU.subtract)
+            for fin in pend:
+                fin()
+            d4 = work.tile([P, S], F32, name="d4")
+            nc.vector.tensor_tensor(d4[:], h_win[t][:].indirect(n4_l[:]), h_flat[t], ALU.subtract)
+            side = work.tile([P, S], F32, name="side")
+            nc.vector.tensor_tensor(side[:], y_win[t][:].indirect(n6_l[:]), d5[:], ALU.mult)
+            own = work.tile([P, S], F32, name="own")
+            nc.vector.tensor_tensor(own[:], d4[:], y_win[t][:, :S], ALU.mult)
+
+            def finish(t=t, side=side, own=own):
+                res = work.tile([P, S], F32, name="res")
+                nc.vector.scalar_tensor_tensor(res[:], side[:], 0.5, own[:], ALU.mult, ALU.add)
+                nc.sync.dma_start(out_rows[t], res[:])
+
+            pend = [finish]
+        for fin in pend:
+            fin()

@@ -1,6 +1,7 @@
 from contextlib import ExitStack
 
 import concourse.mybir as mybir
+from concourse.masks import make_identity
 
 K, T, S, N, H = 512, 2048, 512, 512, 512
 FLOPS = 2 * K * H * S + 2 * H * N * S
@@ -35,15 +36,17 @@ def tile_picked_skipflowblerp_none_p_kernel(
             nc.sync.dma_start(lst[:], src)
             return lst
 
+        xs_all = keep.tile([P, T], U8, name="xs_all")
+        xs_rows = keep.tile([P, T], U8, name="xs_rows")
+        for q in range(4):
+            queue = nc.scalar if q else nc.sync
+            queue.dma_start(
+                xs_rows[32 * q : 32 * q + 4, :].bitcast(I32), x_scales[0, 4 * q : 4 * q + 4, :].bitcast(I32)
+            )
+        offs_l = load_list("offs_l", offs)
         x_all = keep.tile([P, T], U32, name="x_all")
         nc.sync.dma_start(x_all[:].bitcast(I32), x_words[0].rearrange("p n t -> p (n t)").bitcast(I32))
-        offs_l = load_list("offs_l", offs)
-        xs_all = keep.tile([P, T], U8, name="xs_all")
         nc.vector.memset(xs_all[:].bitcast(I32), 0)
-        for q in range(4):
-            nc.scalar.dma_start(
-                xs_all[32 * q : 32 * q + 4, :].bitcast(I32), x_scales[0, 4 * q : 4 * q + 4, :].bitcast(I32)
-            )
         w1_raw = [keep.tile([P, PACK, H // 2], F32, name="w1_raw%d" % c) for c in range(2)]
         for c in range(2):
             nc.sync.dma_start(w1_raw[c][:], w1.rearrange("(p j) c -> p j c", j=PACK)[:, :, c * (H // 2) : (c + 1) * (H // 2)])
@@ -66,9 +69,16 @@ def tile_picked_skipflowblerp_none_p_kernel(
         h_win = [keep.tile([P, WIN], F32, name="h_win%d" % t) for t in range(PACK)]
         h_last = keep.tile([P, S], F32, name="h_last")
         h_flat = [h_win[t + 1][:, S:] for t in range(PACK - 1)] + [h_last[:]]
-        for win in y_win + h_win[:1]:
+        for win in y_win[:2]:
             nc.vector.memset(win[:, S:], 0.0)
+        for win in y_win[2:] + h_win[:1]:
+            nc.gpsimd.memset(win[:, S:], 0.0)
 
+        for q in range(4):
+            rows = slice(32 * q, 32 * q + 4)
+            nc.vector.tensor_copy(xs_all[rows, :].bitcast(I32), xs_rows[rows, :].bitcast(I32))
+        ident = keep.tile([P, P], F32, name="ident")
+        make_identity(nc, ident[:])
         xs_pick = keep.tile([P, S], U8, name="xs_pick", align_bytes=64)
         nc.vector.tensor_copy(xs_pick[:], xs_all[:].indirect(offs_l[:]))
         x_pick = keep.tile([P, S], U32, name="x_pick", align_bytes=64)
@@ -77,11 +87,11 @@ def tile_picked_skipflowblerp_none_p_kernel(
         neg_gain = keep.tile([P, PACK], F32, name="neg_gain")
         nc.vector.tensor_scalar(neg_gain[:], gain[:], -1.0, None, ALU.mult)
 
-        def round_pair(name, raw, u, copy):
-            dealt = keep.tile([P, 2, P, PACK], BF16, name="%s_bf%d" % (name, u), align_bytes=64)
-            src = raw[:].rearrange("p j (m t) -> p m j t", t=PACK)[:, :, :, 2 * u : 2 * u + 2]
+        def round_w2(u, tag, copy):
+            dealt = keep.tile([P, 2, P, PACK], BF16, name="w2_bf%d" % u, tag=tag, align_bytes=64)
+            src = w2_raw[:].rearrange("p j (m t) -> p m j t", t=PACK)[:, :, :, 2 * u : 2 * u + 2]
             copy(dealt[:].rearrange("p t m j -> p m j t"), src)
-            return dealt
+            return quantise("w2_%d" % u, dealt[:].rearrange("p t m j -> p (t m j)"), 2 * P)
 
         def quantise(name, grouped, width):
             codes = keep.tile([P, width], U32, name=name + "_codes", align_bytes=64)
@@ -97,29 +107,32 @@ def tile_picked_skipflowblerp_none_p_kernel(
                 rhs=codes[:].bitcast(FP8X4), rhs_scale=scales[:], start=True, stop=True,
             )
 
-        flat = "p t m j -> p (t m j)"
         w1_bf = [keep.tile([P, 2, P, PACK], BF16, name="w1_bf%d" % u, align_bytes=64) for u in range(2)]
 
         def round_w1(c, u):
             src = w1_raw[c][:].rearrange("p j (m t) -> p m j t", t=PACK)[:, :, :, 2 * u : 2 * u + 2]
             dst = w1_bf[u][:, :, c * (P // 2) : (c + 1) * (P // 2), :]
-            nc.vector.tensor_copy(dst.rearrange("p t m j -> p m j t"), src)
+            copy = nc.scalar.copy if u else nc.vector.tensor_copy
+            copy(dst.rearrange("p t m j -> p m j t"), src)
 
         round_w1(0, 0)
         round_w1(0, 1)
         round_w1(1, 0)
-        w1_q = []
+        y_acc = []
         for t in range(PACK):
             if t == 1:
                 round_w1(1, 1)
-            w1_q.append(quantise("w1_%d" % t, w1_bf[t // 2][:, t % 2].rearrange("p m j -> p (m j)"), P))
-            y_acc = psum.tile([P, S], F32, name="acc")
-            w_codes, w_scales = w1_q[t]
-            nc.tensor.matmul_mx(
-                out=y_acc[:], lhsT=w_codes[:].bitcast(FP8X4), lhsT_scale=w_scales[:],
-                rhs=x_pick[:].bitcast(FP8X4), rhs_scale=xs_pick[:], start=True, stop=True,
-            )
-            nc.scalar.copy(y_win[t][:, :S], y_acc[:])
+            w_codes, w_scales = quantise("w1_%d" % t, w1_bf[t // 2][:, t % 2].rearrange("p m j -> p (m j)"), P)
+            for cols in ([slice(0, HALF), slice(HALF, S)] if t == 0 else [slice(0, S)]):
+                acc = psum.tile([P, cols.stop - cols.start], F32, name="acc")
+                nc.tensor.matmul_mx(
+                    out=acc[:], lhsT=w_codes[:].bitcast(FP8X4), lhsT_scale=w_scales[:],
+                    rhs=x_pick[:, cols].bitcast(FP8X4), rhs_scale=xs_pick[:, cols], start=True, stop=True,
+                )
+                y_acc.append(acc)
+        nc.vector.tensor_copy(y_win[0][:, :HALF], y_acc[0][:])
+        nc.scalar.copy(y_win[0][:, HALF:S], y_acc[1][:])
+        nc.vector.tensor_copy(y_win[1][:, :S], y_acc[2][:])
 
         w2_q = []
 
@@ -148,51 +161,72 @@ def tile_picked_skipflowblerp_none_p_kernel(
                 )
             pend.clear()
 
-        def second(half, planes, copy):
-            z_bf = keep.tile([P, HALF, PACK], BF16, name="z_bf%d" % half, align_bytes=64)
+        def quantise_z(half, copy, tag):
+            z_bf = keep.tile([P, HALF, PACK], BF16, name="z_bf%d" % half, tag=tag, align_bytes=64)
             copy(
                 z_bf[:].rearrange("p (c i) t -> p c t i", i=4),
-                planes.rearrange("p t (c i) -> p c t i", i=4),
+                z_planes[:, :, half * HALF : (half + 1) * HALF].rearrange("p t (c i) -> p c t i", i=4),
             )
-            z_codes, z_scales = quantise("z%d" % half, z_bf[:].rearrange("p c t -> p (c t)"), HALF)
+            return quantise("z%d" % half, z_bf[:].rearrange("p c t -> p (c t)"), HALF)
+
+        def hidden(t, half):
             cols = slice(half * HALF, (half + 1) * HALF)
-            for t in range(PACK):
-                h_acc = psum.tile([P, HALF], F32, name="acc")
-                product(h_acc[:], w2_q, t, z_codes, z_scales)
-                nc.scalar.copy(h_win[t][:, cols], h_acc[:])
-                nc.scalar.copy(h_flat[t][:, cols], h_acc[:])
+            h_acc = psum.tile([P, HALF], F32, name="acc")
+            product(h_acc[:], w2_q, t, z_q[half][0], z_q[half][1])
+            nc.scalar.activation(h_win[t][:, cols], h_acc[:], ACT.Copy, scale=0.5)
+            nc.scalar.activation(h_flat[t][:, cols], h_acc[:], ACT.Copy, scale=0.5)
 
         blend(0, [0])
         blend(0, [1])
         blend(1, [0, 1])
-        w2_bf = [round_pair("w2", w2_raw, 0, nc.vector.tensor_copy), round_pair("w2", w2_raw, 1, nc.scalar.copy)]
-        w2_q.extend([quantise("w2_%d" % u, w2_bf[u][:].rearrange(flat), 2 * P) for u in range(2)])
-        blend(2, [0, 1])
+        nc.scalar.copy(y_win[2][:, :S], y_acc[3][:])
+        blend(2, [0])
+        nc.scalar.copy(y_win[3][:, :S], y_acc[4][:])
         blend(3, [0])
+        w2_q.append(round_w2(0, "w2_bf0", nc.scalar.copy))
+        blend(2, [1])
+        z_q = [quantise_z(0, nc.scalar.copy, "z_bf0")]
         blend(3, [1])
+        hidden(0, 0)
         flush()
-        second(0, z_planes[:, :, :HALF], nc.scalar.copy)
-        second(1, z_planes[:, :, HALF:], nc.vector.tensor_copy)
+        hidden(1, 0)
+        z_q.append(quantise_z(1, nc.vector.tensor_copy, "late_bf"))
+        hidden(0, 1)
+        hidden(1, 1)
+        w2_q.append(round_w2(1, "late_bf", nc.vector.tensor_copy))
+        for t in (2, 3):
+            for half in range(2):
+                hidden(t, half)
 
         out_rows = out.rearrange("(p t) j -> t p j", t=PACK)
-        pend = []
         for t in range(PACK):
             d5 = work.tile([P, S], F32, name="d5")
             nc.vector.tensor_tensor(d5[:], h_win[t][:].indirect(n5_l[:]), h_flat[t], ALU.subtract)
-            for fin in pend:
-                fin()
             d4 = work.tile([P, S], F32, name="d4")
             nc.vector.tensor_tensor(d4[:], h_win[t][:].indirect(n4_l[:]), h_flat[t], ALU.subtract)
             side = work.tile([P, S], F32, name="side")
             nc.vector.tensor_tensor(side[:], y_win[t][:].indirect(n6_l[:]), d5[:], ALU.mult)
             own = work.tile([P, S], F32, name="own")
-            nc.vector.tensor_tensor(own[:], d4[:], y_win[t][:, :S], ALU.mult)
-
-            def finish(t=t, side=side, own=own):
-                res = work.tile([P, S], F32, name="res")
-                nc.vector.scalar_tensor_tensor(res[:], side[:], 0.5, own[:], ALU.mult, ALU.add)
+            nc.vector.scalar_tensor_tensor(own[:], d4[:], 2.0, y_win[t][:, :S], ALU.mult, ALU.mult)
+            res = work.tile([P, S], F32, name="res")
+            if t < PACK - 1:
+                turned = psum.tile([P, S], F32, name="acc")
+                for c in range(S // P):
+                    cols = slice(c * P, (c + 1) * P)
+                    for k, term in enumerate((side, own)):
+                        nc.tensor.matmul(
+                            turned[:, cols], term[:, cols], ident[:], start=(k == 0), stop=(k == 1), is_transpose=True
+                        )
+                total = work.tile([P, S], F32, name="total")
+                nc.scalar.copy(total[:], turned[:])
+                back = psum.tile([P, S], F32, name="acc")
+                for c in range(S // P):
+                    cols = slice(c * P, (c + 1) * P)
+                    nc.tensor.transpose(back[:, cols], total[:, cols], ident[:])
+                nc.scalar.copy(res[:], back[:])
                 nc.sync.dma_start(out_rows[t], res[:])
-
-            pend = [finish]
-        for fin in pend:
-            fin()
+            else:
+                for half in range(2):
+                    cols = slice(half * HALF, (half + 1) * HALF)
+                    nc.vector.tensor_tensor(res[:, cols], side[:, cols], own[:, cols], ALU.add)
+                    nc.sync.dma_start(out_rows[t][:, cols], res[:, cols])

@@ -18,38 +18,53 @@ ALU = mybir.AluOpType
 
 P = 128
 PACK = 4
+GROUP = 16
+QUADRANT = 32
 HALF = S // 2
-WIN = 2 * S
+WINDOW = 2 * S
+
+
+def pieces(cols, n):
+    step = (cols.stop - cols.start) // n
+    return [slice(cols.start + k * step, cols.start + (k + 1) * step) for k in range(n)]
+
+
+def entries(lst, cols):
+    return lst[:, cols.start // GROUP : cols.stop // GROUP]
 
 
 def tile_picked_skipflowblerp_none_p_kernel(
     tc, x_words, x_scales, w1, gn, w2, offs, n1, n2, n3, n4, n5, n6, out
 ):
     nc = tc.nc
+    whole = slice(0, S)
+    halves = pieces(whole, 2)
+
     with ExitStack() as ctx:
         keep = ctx.enter_context(tc.tile_pool(name="keep", bufs=1))
-        work = ctx.enter_context(tc.tile_pool(name="work", bufs=4))
+        work = ctx.enter_context(tc.tile_pool(name="work", bufs=PACK))
         psum = ctx.enter_context(tc.psum_pool(name="psum", bufs=8))
 
         def load_list(name, src):
-            lst = keep.tile([P, S // 16], U16, name=name)
+            lst = keep.tile([P, S // GROUP], U16, name=name)
             nc.sync.dma_start(lst[:], src)
             return lst
 
         xs_all = keep.tile([P, T], U8, name="xs_all")
-        xs_rows = keep.tile([P, T], U8, name="xs_rows")
-        for q in range(4):
-            queue = nc.scalar if q else nc.sync
-            queue.dma_start(
-                xs_rows[32 * q : 32 * q + 4, :].bitcast(I32), x_scales[0, 4 * q : 4 * q + 4, :].bitcast(I32)
-            )
         offs_l = load_list("offs_l", offs)
+        xs_rows = keep.tile([P, T], U8, name="xs_rows")
+        scale_rows = [slice(QUADRANT * q, QUADRANT * q + PACK) for q in range(P // QUADRANT)]
+        for q, queue in enumerate((nc.sync, nc.sync, nc.scalar, nc.scalar)):
+            queue.dma_start(
+                xs_rows[scale_rows[q], :].bitcast(I32), x_scales[0, PACK * q : PACK * (q + 1), :].bitcast(I32)
+            )
         x_all = keep.tile([P, T], U32, name="x_all")
-        nc.sync.dma_start(x_all[:].bitcast(I32), x_words[0].rearrange("p n t -> p (n t)").bitcast(I32))
+        nc.sync.dma_start(x_all[:].bitcast(I32), x_words[0].rearrange("p n j -> p (n j)").bitcast(I32))
         nc.vector.memset(xs_all[:].bitcast(I32), 0)
+        w1_rows = w1.rearrange("(p j) c -> p j c", j=PACK)
         w1_raw = [keep.tile([P, PACK, H // 2], F32, name="w1_raw%d" % c) for c in range(2)]
-        for c in range(2):
-            nc.sync.dma_start(w1_raw[c][:], w1.rearrange("(p j) c -> p j c", j=PACK)[:, :, c * (H // 2) : (c + 1) * (H // 2)])
+        for raw, cols in zip(w1_raw, pieces(slice(0, H), 2)):
+            nc.sync.dma_start(raw[:], w1_rows[:, :, cols])
         n2_l = load_list("n2_l", n2)
         n3_l = load_list("n3_l", n3)
         n1_l = load_list("n1_l", n1)
@@ -61,21 +76,21 @@ def tile_picked_skipflowblerp_none_p_kernel(
         n5_l = load_list("n5_l", n5)
         n6_l = load_list("n6_l", n6)
 
-        warm = keep.tile([P, 2], F32, name="warm")
-        nc.vector.memset(warm[:, 0:1], 0.0)
-        nc.scalar.activation(warm[:, 1:2], warm[:, 0:1], ACT.Sigmoid)
+        const = keep.tile([P, 2], F32, name="const")
+        nc.vector.memset(const[:, 0:1], 0.0)
+        nc.scalar.activation(const[:, 1:2], const[:, 0:1], ACT.Sigmoid)
+        one_half = const[:, 1:2]
 
-        y_win = [keep.tile([P, WIN], F32, name="y_win%d" % t) for t in range(PACK)]
-        h_win = [keep.tile([P, WIN], F32, name="h_win%d" % t) for t in range(PACK)]
+        y_win = [keep.tile([P, WINDOW], F32, name="y_win%d" % t) for t in range(PACK)]
+        h_win = [keep.tile([P, WINDOW], F32, name="h_win%d" % t) for t in range(PACK)]
         h_last = keep.tile([P, S], F32, name="h_last")
-        h_flat = [h_win[t + 1][:, S:] for t in range(PACK - 1)] + [h_last[:]]
+        h_plain = [win[:, S:] for win in h_win[1:]] + [h_last[:]]
         for win in y_win[:2]:
             nc.vector.memset(win[:, S:], 0.0)
         for win in y_win[2:] + h_win[:1]:
             nc.gpsimd.memset(win[:, S:], 0.0)
 
-        for q in range(4):
-            rows = slice(32 * q, 32 * q + 4)
+        for rows in scale_rows:
             nc.vector.tensor_copy(xs_all[rows, :].bitcast(I32), xs_rows[rows, :].bitcast(I32))
         ident = keep.tile([P, P], F32, name="ident")
         make_identity(nc, ident[:])
@@ -85,13 +100,7 @@ def tile_picked_skipflowblerp_none_p_kernel(
         nc.vector.tensor_copy(x_pick[:], x_all[:].indirect(offs_l[:]))
 
         neg_gain = keep.tile([P, PACK], F32, name="neg_gain")
-        nc.vector.tensor_scalar(neg_gain[:], gain[:], -1.0, None, ALU.mult)
-
-        def round_w2(u, tag, copy):
-            dealt = keep.tile([P, 2, P, PACK], BF16, name="w2_bf%d" % u, tag=tag, align_bytes=64)
-            src = w2_raw[:].rearrange("p j (m t) -> p m j t", t=PACK)[:, :, :, 2 * u : 2 * u + 2]
-            copy(dealt[:].rearrange("p t m j -> p m j t"), src)
-            return quantise("w2_%d" % u, dealt[:].rearrange("p t m j -> p (t m j)"), 2 * P)
+        nc.gpsimd.tensor_scalar(neg_gain[:], gain[:], -1.0, 0.0, ALU.mult, ALU.add)
 
         def quantise(name, grouped, width):
             codes = keep.tile([P, width], U32, name=name + "_codes", align_bytes=64)
@@ -99,134 +108,152 @@ def tile_picked_skipflowblerp_none_p_kernel(
             nc.vector.quantize_mx(out=codes[:].bitcast(FP8X4), scales=scales[:], in_=grouped)
             return codes, scales
 
-        def product(acc, weights, t, codes, scales):
-            w_codes, w_scales = weights[t // 2]
-            cols = slice((t % 2) * P, (t % 2 + 1) * P)
+        def product(acc, w_codes, w_scales, codes, scales):
             nc.tensor.matmul_mx(
-                out=acc, lhsT=w_codes[:, cols].bitcast(FP8X4), lhsT_scale=w_scales[:, cols],
-                rhs=codes[:].bitcast(FP8X4), rhs_scale=scales[:], start=True, stop=True,
+                out=acc, lhsT=w_codes.bitcast(FP8X4), lhsT_scale=w_scales,
+                rhs=codes.bitcast(FP8X4), rhs_scale=scales, start=True, stop=True,
             )
 
-        w1_bf = [keep.tile([P, 2, P, PACK], BF16, name="w1_bf%d" % u, align_bytes=64) for u in range(2)]
+        def deal(copy, dealt, raw, pair):
+            src = raw.rearrange("p j (m t) -> p m j t", t=PACK)[:, :, :, 2 * pair : 2 * pair + 2]
+            copy(dealt.rearrange("p t m j -> p m j t"), src)
 
-        def round_w1(c, u):
-            src = w1_raw[c][:].rearrange("p j (m t) -> p m j t", t=PACK)[:, :, :, 2 * u : 2 * u + 2]
-            dst = w1_bf[u][:, :, c * (P // 2) : (c + 1) * (P // 2), :]
-            copy = nc.scalar.copy if u else nc.vector.tensor_copy
-            copy(dst.rearrange("p t m j -> p m j t"), src)
+        w1_bf = [keep.tile([P, 2, P, PACK], BF16, name="w1_bf%d" % pair, align_bytes=64) for pair in range(2)]
+        first_m, second_m = pieces(slice(0, P), 2)
 
-        round_w1(0, 0)
-        round_w1(0, 1)
-        round_w1(1, 0)
-        y_acc = []
-        for t in range(PACK):
-            if t == 1:
-                round_w1(1, 1)
+        def project(t, parts):
             w_codes, w_scales = quantise("w1_%d" % t, w1_bf[t // 2][:, t % 2].rearrange("p m j -> p (m j)"), P)
-            for cols in ([slice(0, HALF), slice(HALF, S)] if t == 0 else [slice(0, S)]):
+            banks = []
+            for cols in parts:
                 acc = psum.tile([P, cols.stop - cols.start], F32, name="acc")
-                nc.tensor.matmul_mx(
-                    out=acc[:], lhsT=w_codes[:].bitcast(FP8X4), lhsT_scale=w_scales[:],
-                    rhs=x_pick[:, cols].bitcast(FP8X4), rhs_scale=xs_pick[:, cols], start=True, stop=True,
-                )
-                y_acc.append(acc)
-        nc.vector.tensor_copy(y_win[0][:, :HALF], y_acc[0][:])
-        nc.scalar.copy(y_win[0][:, HALF:S], y_acc[1][:])
-        nc.vector.tensor_copy(y_win[1][:, :S], y_acc[2][:])
+                product(acc[:], w_codes[:], w_scales[:], x_pick[:, cols], xs_pick[:, cols])
+                banks.append(acc)
+            return banks
 
-        w2_q = []
+        deal(nc.scalar.copy, w1_bf[0][:, :, first_m, :], w1_raw[0][:], 0)
+        deal(nc.scalar.copy, w1_bf[1][:, :, first_m, :], w1_raw[0][:], 1)
+        deal(nc.vector.tensor_copy, w1_bf[0][:, :, second_m, :], w1_raw[1][:], 0)
+        y_acc = [project(0, halves)]
+        deal(nc.scalar.copy, w1_bf[1][:, :, second_m, :], w1_raw[1][:], 1)
+        y_acc.extend([project(t, [whole]) for t in range(1, PACK)])
+        nc.vector.tensor_copy(y_win[0][:, halves[0]], y_acc[0][0][:])
+        nc.scalar.copy(y_win[0][:, halves[1]], y_acc[0][1][:])
+        nc.vector.tensor_copy(y_win[1][:, whole], y_acc[1][0][:])
 
         z_planes = keep.tile([P, PACK, S], BF16, name="z_planes")
-        pend = []
+        waiting = []
 
-        def blend(t, halves):
-            width = HALF * len(halves)
-            cols = slice(halves[0] * HALF // 16, (halves[-1] + 1) * HALF // 16)
+        def blend(t, cols, near_pieces=1):
+            width = cols.stop - cols.start
             gate = work.tile([P, width], F32, name="gate")
-            nc.scalar.activation(gate[:], y_win[t][:].indirect(n2_l[:, cols]), ACT.Sigmoid)
+            nc.scalar.activation(gate[:], y_win[t][:].indirect(entries(n2_l, cols)), ACT.Sigmoid)
             rest = work.tile([P, width], F32, name="rest")
             nc.scalar.activation(rest[:], gate[:], ACT.Identity, bias=gain[:, t : t + 1], scale=neg_gain[:, t : t + 1])
             far = work.tile([P, width], F32, name="far")
-            nc.vector.tensor_tensor(far[:], y_win[t][:].indirect(n3_l[:, cols]), gate[:], ALU.mult)
-            flush()
+            nc.vector.tensor_tensor(far[:], y_win[t][:].indirect(entries(n3_l, cols)), gate[:], ALU.mult)
+            add_waiting()
             near = work.tile([P, width], F32, name="near")
-            nc.vector.tensor_tensor(near[:], y_win[t][:].indirect(n1_l[:, cols]), rest[:], ALU.mult)
-            pend.append((t, halves, far, near))
-
-        def flush():
-            for t, halves, far, near in pend:
-                part = slice(halves[0] * HALF, (halves[-1] + 1) * HALF)
-                nc.vector.scalar_tensor_tensor(
-                    z_planes[:, t, part], far[:], gain[:, t : t + 1], near[:], ALU.mult, ALU.add
+            for local, part in zip(pieces(slice(0, width), near_pieces), pieces(cols, near_pieces)):
+                nc.vector.tensor_tensor(
+                    near[:, local], y_win[t][:].indirect(entries(n1_l, part)), rest[:, local], ALU.mult
                 )
-            pend.clear()
+                waiting.append((t, part, far[:, local], near[:, local]))
 
-        def quantise_z(half, copy, tag):
+        def add_waiting():
+            for t, part, far, near in waiting:
+                nc.vector.scalar_tensor_tensor(z_planes[:, t, part], far, gain[:, t : t + 1], near, ALU.mult, ALU.add)
+            waiting.clear()
+
+        def quantise_z(half, copies, tag):
             z_bf = keep.tile([P, HALF, PACK], BF16, name="z_bf%d" % half, tag=tag, align_bytes=64)
-            copy(
-                z_bf[:].rearrange("p (c i) t -> p c t i", i=4),
-                z_planes[:, :, half * HALF : (half + 1) * HALF].rearrange("p t (c i) -> p c t i", i=4),
-            )
+            shares = zip(copies, pieces(slice(0, HALF), len(copies)), pieces(halves[half], len(copies)))
+            for copy, local, part in shares:
+                copy(
+                    z_bf[:, local, :].rearrange("p (c i) t -> p c t i", i=4),
+                    z_planes[:, :, part].rearrange("p t (c i) -> p c t i", i=4),
+                )
             return quantise("z%d" % half, z_bf[:].rearrange("p c t -> p (c t)"), HALF)
 
-        def hidden(t, half):
-            cols = slice(half * HALF, (half + 1) * HALF)
-            h_acc = psum.tile([P, HALF], F32, name="acc")
-            product(h_acc[:], w2_q, t, z_q[half][0], z_q[half][1])
-            nc.scalar.activation(h_win[t][:, cols], h_acc[:], ACT.Copy, scale=0.5)
-            nc.scalar.activation(h_flat[t][:, cols], h_acc[:], ACT.Copy, scale=0.5)
+        def quantise_w2(pair, copy, tag):
+            dealt = keep.tile([P, 2, P, PACK], BF16, name="w2_bf%d" % pair, tag=tag, align_bytes=64)
+            deal(copy, dealt[:], w2_raw[:], pair)
+            return quantise("w2_%d" % pair, dealt[:].rearrange("p t m j -> p (t m j)"), 2 * P)
 
-        blend(0, [0])
-        blend(0, [1])
-        blend(1, [0, 1])
-        nc.scalar.copy(y_win[2][:, :S], y_acc[3][:])
-        blend(2, [0])
-        nc.scalar.copy(y_win[3][:, :S], y_acc[4][:])
-        blend(3, [0])
-        w2_q.append(round_w2(0, "w2_bf0", nc.scalar.copy))
-        blend(2, [1])
-        z_q = [quantise_z(0, nc.scalar.copy, "z_bf0")]
-        blend(3, [1])
-        hidden(0, 0)
-        flush()
-        hidden(1, 0)
-        z_q.append(quantise_z(1, nc.vector.tensor_copy, "late_bf"))
-        hidden(0, 1)
-        hidden(1, 1)
-        w2_q.append(round_w2(1, "late_bf", nc.vector.tensor_copy))
-        for t in (2, 3):
-            for half in range(2):
-                hidden(t, half)
+        def hidden(t):
+            w_codes, w_scales = w2_q[t // 2]
+            m = pieces(slice(0, 2 * P), 2)[t % 2]
+            for cols, (z_codes, z_scales) in zip(halves, z_q):
+                acc = psum.tile([P, HALF], F32, name="acc")
+                product(acc[:], w_codes[:, m], w_scales[:, m], z_codes[:], z_scales[:])
+                nc.scalar.activation(h_win[t][:, cols], acc[:], ACT.Copy, scale=one_half)
+                nc.scalar.activation(h_plain[t][:, cols], acc[:], ACT.Copy, scale=one_half)
+
+        blend(0, halves[0])
+        blend(0, halves[1])
+        blend(1, whole)
+        nc.scalar.copy(y_win[2][:, whole], y_acc[2][0][:])
+        blend(2, halves[0])
+        nc.scalar.copy(y_win[3][:, whole], y_acc[3][0][:])
+        blend(3, halves[0])
+        w2_q = [quantise_w2(0, nc.scalar.copy, "w2_bf0")]
+        blend(2, halves[1])
+        z_q = [quantise_z(0, [nc.scalar.copy], "z_bf0")]
+        blend(3, halves[1], near_pieces=2)
+        add_waiting()
+        z_q.append(quantise_z(1, [nc.scalar.copy, nc.vector.tensor_copy], "late_bf"))
+
+        hidden(0)
+        hidden(1)
+        w2_q.append(quantise_w2(1, nc.vector.tensor_copy, "late_bf"))
+        hidden(2)
+        hidden(3)
 
         out_rows = out.rearrange("(p t) j -> t p j", t=PACK)
-        for t in range(PACK):
-            d5 = work.tile([P, S], F32, name="d5")
-            nc.vector.tensor_tensor(d5[:], h_win[t][:].indirect(n5_l[:]), h_flat[t], ALU.subtract)
-            d4 = work.tile([P, S], F32, name="d4")
-            nc.vector.tensor_tensor(d4[:], h_win[t][:].indirect(n4_l[:]), h_flat[t], ALU.subtract)
-            side = work.tile([P, S], F32, name="side")
-            nc.vector.tensor_tensor(side[:], y_win[t][:].indirect(n6_l[:]), d5[:], ALU.mult)
-            own = work.tile([P, S], F32, name="own")
-            nc.vector.scalar_tensor_tensor(own[:], d4[:], 2.0, y_win[t][:, :S], ALU.mult, ALU.mult)
-            res = work.tile([P, S], F32, name="res")
-            if t < PACK - 1:
-                turned = psum.tile([P, S], F32, name="acc")
-                for c in range(S // P):
-                    cols = slice(c * P, (c + 1) * P)
-                    for k, term in enumerate((side, own)):
-                        nc.tensor.matmul(
-                            turned[:, cols], term[:, cols], ident[:], start=(k == 0), stop=(k == 1), is_transpose=True
-                        )
-                total = work.tile([P, S], F32, name="total")
-                nc.scalar.copy(total[:], turned[:])
-                back = psum.tile([P, S], F32, name="acc")
-                for c in range(S // P):
-                    cols = slice(c * P, (c + 1) * P)
-                    nc.tensor.transpose(back[:, cols], total[:, cols], ident[:])
-                nc.scalar.copy(res[:], back[:])
-                nc.sync.dma_start(out_rows[t], res[:])
-            else:
-                for half in range(2):
-                    cols = slice(half * HALF, (half + 1) * HALF)
-                    nc.vector.tensor_tensor(res[:, cols], side[:, cols], own[:, cols], ALU.add)
-                    nc.sync.dma_start(out_rows[t][:, cols], res[:, cols])
+        blocks = pieces(whole, S // P)
+
+        def terms():
+            return [work.tile([P, S], F32, name=name) for name in ("d5", "d4", "side", "own", "res")]
+
+        def difference(dst, lst, t, cols):
+            nc.vector.tensor_tensor(
+                dst[:, cols], h_win[t][:].indirect(entries(lst, cols)), h_plain[t][:, cols], ALU.subtract
+            )
+
+        def side_term(side, d5, t, cols):
+            nc.vector.tensor_tensor(side[:, cols], y_win[t][:].indirect(entries(n6_l, cols)), d5[:, cols], ALU.mult)
+
+        def own_term(own, d4, t):
+            nc.vector.scalar_tensor_tensor(own[:], d4[:], 2.0, y_win[t][:, whole], ALU.mult, ALU.mult)
+
+        for t in range(PACK - 1):
+            d5, d4, side, own, res = terms()
+            for cols in halves if t == 0 else [whole]:
+                difference(d5, n5_l, t, cols)
+            difference(d4, n4_l, t, whole)
+            side_term(side, d5, t, whole)
+            own_term(own, d4, t)
+            turned = psum.tile([P, S], F32, name="acc")
+            steps = [(term, cols) for term in (side, own) for cols in blocks]
+            for k, (term, cols) in enumerate(steps):
+                nc.tensor.matmul(
+                    turned[:, cols], term[:, cols], ident[:],
+                    start=(k == 0), stop=(k == len(steps) - 1), is_transpose=True,
+                )
+            total = work.tile([P, S], F32, name="total")
+            nc.scalar.copy(total[:], turned[:])
+            back = psum.tile([P, S], F32, name="acc")
+            for cols in blocks:
+                nc.tensor.transpose(back[:, cols], total[:, cols], ident[:])
+            nc.scalar.copy(res[:], back[:])
+            nc.sync.dma_start(out_rows[t], res[:])
+
+        last = PACK - 1
+        d5, d4, side, own, res = terms()
+        difference(d4, n4_l, last, whole)
+        difference(d5, n5_l, last, whole)
+        own_term(own, d4, last)
+        for cols in halves:
+            side_term(side, d5, last, cols)
+        for cols in halves:
+            nc.vector.tensor_tensor(res[:, cols], side[:, cols], own[:, cols], ALU.add)
+            nc.sync.dma_start(out_rows[last][:, cols], res[:, cols])

from contextlib import ExitStack

import concourse.mybir as mybir
from concourse.masks import make_identity

K, T, S, N, H = 512, 2048, 512, 512, 512
FLOPS = 2 * K * H * S + 2 * H * N * S

F32 = mybir.dt.float32
BF16 = mybir.dt.bfloat16
I32 = mybir.dt.int32
U32 = mybir.dt.uint32
U16 = mybir.dt.uint16
U8 = mybir.dt.uint8
FP8X4 = mybir.dt.float8_e4m3fn_x4
ACT = mybir.ActivationFunctionType
ALU = mybir.AluOpType

P = 128
PACK = 4
GROUP = 16
QUADRANT = 32
HALF = S // 2
WINDOW = 2 * S


def pieces(cols, n):
    step = (cols.stop - cols.start) // n
    return [slice(cols.start + k * step, cols.start + (k + 1) * step) for k in range(n)]


def entries(lst, cols):
    return lst[:, cols.start // GROUP : cols.stop // GROUP]


def tile_picked_skipflowblerp_none_p_kernel(
    tc, x_words, x_scales, w1, gn, w2, offs, n1, n2, n3, n4, n5, n6, out
):
    nc = tc.nc
    whole = slice(0, S)
    halves = pieces(whole, 2)

    with ExitStack() as ctx:
        keep = ctx.enter_context(tc.tile_pool(name="keep", bufs=1))
        work = ctx.enter_context(tc.tile_pool(name="work", bufs=PACK))
        psum = ctx.enter_context(tc.psum_pool(name="psum", bufs=8))

        def load_list(name, src):
            lst = keep.tile([P, S // GROUP], U16, name=name)
            nc.sync.dma_start(lst[:], src)
            return lst

        xs_all = keep.tile([P, T], U8, name="xs_all")
        offs_l = load_list("offs_l", offs)
        xs_rows = keep.tile([P, T], U8, name="xs_rows")
        scale_rows = [slice(QUADRANT * q, QUADRANT * q + PACK) for q in range(P // QUADRANT)]
        for q, queue in enumerate((nc.sync, nc.sync, nc.scalar, nc.scalar)):
            queue.dma_start(
                xs_rows[scale_rows[q], :].bitcast(I32), x_scales[0, PACK * q : PACK * (q + 1), :].bitcast(I32)
            )
        x_all = keep.tile([P, T], U32, name="x_all")
        nc.sync.dma_start(x_all[:].bitcast(I32), x_words[0].rearrange("p n j -> p (n j)").bitcast(I32))
        nc.vector.memset(xs_all[:].bitcast(I32), 0)
        w1_rows = w1.rearrange("(p j) c -> p j c", j=PACK)
        w1_raw = [keep.tile([P, PACK, H // 2], F32, name="w1_raw%d" % c) for c in range(2)]
        for raw, cols in zip(w1_raw, pieces(slice(0, H), 2)):
            nc.sync.dma_start(raw[:], w1_rows[:, :, cols])
        n2_l = load_list("n2_l", n2)
        n3_l = load_list("n3_l", n3)
        n1_l = load_list("n1_l", n1)
        gain = keep.tile([P, PACK], F32, name="gain")
        nc.sync.dma_start(gain[:], gn.rearrange("(p t) o -> p (t o)", t=PACK))
        w2_raw = keep.tile([P, PACK, N], F32, name="w2_raw")
        nc.sync.dma_start(w2_raw[:], w2.rearrange("(p j) c -> p j c", j=PACK))
        n4_l = load_list("n4_l", n4)
        n5_l = load_list("n5_l", n5)
        n6_l = load_list("n6_l", n6)

        const = keep.tile([P, 2], F32, name="const")
        nc.vector.memset(const[:, 0:1], 0.0)
        nc.scalar.activation(const[:, 1:2], const[:, 0:1], ACT.Sigmoid)
        one_half = const[:, 1:2]

        y_win = [keep.tile([P, WINDOW], F32, name="y_win%d" % t) for t in range(PACK)]
        h_win = [keep.tile([P, WINDOW], F32, name="h_win%d" % t) for t in range(PACK)]
        h_last = keep.tile([P, S], F32, name="h_last")
        h_plain = [win[:, S:] for win in h_win[1:]] + [h_last[:]]
        for win in y_win[:2]:
            nc.vector.memset(win[:, S:], 0.0)
        for win in y_win[2:] + h_win[:1]:
            nc.gpsimd.memset(win[:, S:], 0.0)

        for rows in scale_rows:
            nc.vector.tensor_copy(xs_all[rows, :].bitcast(I32), xs_rows[rows, :].bitcast(I32))
        ident = keep.tile([P, P], F32, name="ident")
        make_identity(nc, ident[:])
        xs_pick = keep.tile([P, S], U8, name="xs_pick", align_bytes=64)
        nc.vector.tensor_copy(xs_pick[:], xs_all[:].indirect(offs_l[:]))
        x_pick = keep.tile([P, S], U32, name="x_pick", align_bytes=64)
        nc.vector.tensor_copy(x_pick[:], x_all[:].indirect(offs_l[:]))

        neg_gain = keep.tile([P, PACK], F32, name="neg_gain")
        nc.gpsimd.tensor_scalar(neg_gain[:], gain[:], -1.0, 0.0, ALU.mult, ALU.add)

        def quantise(name, grouped, width):
            codes = keep.tile([P, width], U32, name=name + "_codes", align_bytes=64)
            scales = keep.tile([P, width], U8, name=name + "_scales", align_bytes=64)
            nc.vector.quantize_mx(out=codes[:].bitcast(FP8X4), scales=scales[:], in_=grouped)
            return codes, scales

        def product(acc, w_codes, w_scales, codes, scales):
            nc.tensor.matmul_mx(
                out=acc, lhsT=w_codes.bitcast(FP8X4), lhsT_scale=w_scales,
                rhs=codes.bitcast(FP8X4), rhs_scale=scales, start=True, stop=True,
            )

        def deal(copy, dealt, raw, pair):
            src = raw.rearrange("p j (m t) -> p m j t", t=PACK)[:, :, :, 2 * pair : 2 * pair + 2]
            copy(dealt.rearrange("p t m j -> p m j t"), src)

        w1_bf = [keep.tile([P, 2, P, PACK], BF16, name="w1_bf%d" % pair, align_bytes=64) for pair in range(2)]
        first_m, second_m = pieces(slice(0, P), 2)

        def project(t, parts):
            w_codes, w_scales = quantise("w1_%d" % t, w1_bf[t // 2][:, t % 2].rearrange("p m j -> p (m j)"), P)
            banks = []
            for cols in parts:
                acc = psum.tile([P, cols.stop - cols.start], F32, name="acc")
                product(acc[:], w_codes[:], w_scales[:], x_pick[:, cols], xs_pick[:, cols])
                banks.append(acc)
            return banks

        deal(nc.scalar.copy, w1_bf[0][:, :, first_m, :], w1_raw[0][:], 0)
        deal(nc.scalar.copy, w1_bf[1][:, :, first_m, :], w1_raw[0][:], 1)
        deal(nc.vector.tensor_copy, w1_bf[0][:, :, second_m, :], w1_raw[1][:], 0)
        y_acc = [project(0, halves)]
        deal(nc.scalar.copy, w1_bf[1][:, :, second_m, :], w1_raw[1][:], 1)
        y_acc.extend([project(t, [whole]) for t in range(1, PACK)])
        nc.vector.tensor_copy(y_win[0][:, halves[0]], y_acc[0][0][:])
        nc.scalar.copy(y_win[0][:, halves[1]], y_acc[0][1][:])
        nc.vector.tensor_copy(y_win[1][:, whole], y_acc[1][0][:])

        z_planes = keep.tile([P, PACK, S], BF16, name="z_planes")
        waiting = []

        def blend(t, cols, near_pieces=1):
            width = cols.stop - cols.start
            gate = work.tile([P, width], F32, name="gate")
            nc.scalar.activation(gate[:], y_win[t][:].indirect(entries(n2_l, cols)), ACT.Sigmoid)
            rest = work.tile([P, width], F32, name="rest")
            nc.scalar.activation(rest[:], gate[:], ACT.Identity, bias=gain[:, t : t + 1], scale=neg_gain[:, t : t + 1])
            far = work.tile([P, width], F32, name="far")
            nc.vector.tensor_tensor(far[:], y_win[t][:].indirect(entries(n3_l, cols)), gate[:], ALU.mult)
            add_waiting()
            near = work.tile([P, width], F32, name="near")
            for local, part in zip(pieces(slice(0, width), near_pieces), pieces(cols, near_pieces)):
                nc.vector.tensor_tensor(
                    near[:, local], y_win[t][:].indirect(entries(n1_l, part)), rest[:, local], ALU.mult
                )
                waiting.append((t, part, far[:, local], near[:, local]))

        def add_waiting():
            for t, part, far, near in waiting:
                nc.vector.scalar_tensor_tensor(z_planes[:, t, part], far, gain[:, t : t + 1], near, ALU.mult, ALU.add)
            waiting.clear()

        def quantise_z(half, copies, tag):
            z_bf = keep.tile([P, HALF, PACK], BF16, name="z_bf%d" % half, tag=tag, align_bytes=64)
            shares = zip(copies, pieces(slice(0, HALF), len(copies)), pieces(halves[half], len(copies)))
            for copy, local, part in shares:
                copy(
                    z_bf[:, local, :].rearrange("p (c i) t -> p c t i", i=4),
                    z_planes[:, :, part].rearrange("p t (c i) -> p c t i", i=4),
                )
            return quantise("z%d" % half, z_bf[:].rearrange("p c t -> p (c t)"), HALF)

        def quantise_w2(pair, copy, tag):
            dealt = keep.tile([P, 2, P, PACK], BF16, name="w2_bf%d" % pair, tag=tag, align_bytes=64)
            deal(copy, dealt[:], w2_raw[:], pair)
            return quantise("w2_%d" % pair, dealt[:].rearrange("p t m j -> p (t m j)"), 2 * P)

        def hidden(t):
            w_codes, w_scales = w2_q[t // 2]
            m = pieces(slice(0, 2 * P), 2)[t % 2]
            for cols, (z_codes, z_scales) in zip(halves, z_q):
                acc = psum.tile([P, HALF], F32, name="acc")
                product(acc[:], w_codes[:, m], w_scales[:, m], z_codes[:], z_scales[:])
                nc.scalar.activation(h_win[t][:, cols], acc[:], ACT.Copy, scale=one_half)
                nc.scalar.activation(h_plain[t][:, cols], acc[:], ACT.Copy, scale=one_half)

        blend(0, halves[0])
        blend(0, halves[1])
        blend(1, whole)
        nc.scalar.copy(y_win[2][:, whole], y_acc[2][0][:])
        blend(2, halves[0])
        nc.scalar.copy(y_win[3][:, whole], y_acc[3][0][:])
        blend(3, halves[0])
        w2_q = [quantise_w2(0, nc.scalar.copy, "w2_bf0")]
        blend(2, halves[1])
        z_q = [quantise_z(0, [nc.scalar.copy], "z_bf0")]
        blend(3, halves[1], near_pieces=2)
        add_waiting()
        z_q.append(quantise_z(1, [nc.scalar.copy, nc.vector.tensor_copy], "late_bf"))

        hidden(0)
        hidden(1)
        w2_q.append(quantise_w2(1, nc.vector.tensor_copy, "late_bf"))
        hidden(2)
        hidden(3)

        out_rows = out.rearrange("(p t) j -> t p j", t=PACK)
        blocks = pieces(whole, S // P)

        def terms():
            return [work.tile([P, S], F32, name=name) for name in ("d5", "d4", "side", "own", "res")]

        def difference(dst, lst, t, cols):
            nc.vector.tensor_tensor(
                dst[:, cols], h_win[t][:].indirect(entries(lst, cols)), h_plain[t][:, cols], ALU.subtract
            )

        def side_term(side, d5, t, cols):
            nc.vector.tensor_tensor(side[:, cols], y_win[t][:].indirect(entries(n6_l, cols)), d5[:, cols], ALU.mult)

        def own_term(own, d4, t):
            nc.vector.scalar_tensor_tensor(own[:], d4[:], 2.0, y_win[t][:, whole], ALU.mult, ALU.mult)

        for t in range(PACK - 1):
            d5, d4, side, own, res = terms()
            for cols in halves if t == 0 else [whole]:
                difference(d5, n5_l, t, cols)
            difference(d4, n4_l, t, whole)
            side_term(side, d5, t, whole)
            own_term(own, d4, t)
            turned = psum.tile([P, S], F32, name="acc")
            steps = [(term, cols) for term in (side, own) for cols in blocks]
            for k, (term, cols) in enumerate(steps):
                nc.tensor.matmul(
                    turned[:, cols], term[:, cols], ident[:],
                    start=(k == 0), stop=(k == len(steps) - 1), is_transpose=True,
                )
            total = work.tile([P, S], F32, name="total")
            nc.scalar.copy(total[:], turned[:])
            back = psum.tile([P, S], F32, name="acc")
            for cols in blocks:
                nc.tensor.transpose(back[:, cols], total[:, cols], ident[:])
            nc.scalar.copy(res[:], back[:])
            nc.sync.dma_start(out_rows[t], res[:])

        last = PACK - 1
        d5, d4, side, own, res = terms()
        difference(d4, n4_l, last, whole)
        difference(d5, n5_l, last, whole)
        own_term(own, d4, last)
        for cols in halves:
            side_term(side, d5, last, cols)
        for cols in halves:
            nc.vector.tensor_tensor(res[:, cols], side[:, cols], own[:, cols], ALU.add)
            nc.sync.dma_start(out_rows[last][:, cols], res[:, cols])
